import numpy as np, ml_dtypes
CORES = [1,3,5,9,11,13]
N = 6
import mx_ref
NC, G, D = 128, 4, 8
C = np.float32(0.031)
BF = ml_dtypes.bfloat16
def cut(t, i, w=512):
    return t[:, w * i:w * i + w]
def tile(rs):
    return np.stack(rs, axis=2).reshape(128, -1).astype(BF)
def act(Z):
    return [np.maximum(z, 0) * C for z in Z]
def taps(w, i, e):
    return mx_ref.matmul(mx_ref.quantize(cut(w, 2 * i)), mx_ref.quantize(e[:, :4 * NC])) + mx_ref.matmul(mx_ref.quantize(cut(w, 2 * i + 1)), mx_ref.quantize(e[:, 4 * D:4 * D + 4 * NC]))
def setup_inputs(rng):
    def f(*shape):
        return mx_ref.flush((rng.standard_normal(shape, dtype=np.float32) * np.exp2(rng.integers(-2, 3, shape[:-1] + (1,)))).astype(BF))
    return {"x": f(N, 128, 4 * NC), "wa": np.broadcast_to(f(1, 128, 2 * G * 512), (N, 128, 2 * G * 512)).copy(), "wb": f(N, 128, 2 * 512)}
def setup_inputs_blocks(rng):
    d = setup_inputs(rng)
    for k in ("x", "wb"): d[k] = mx_ref.spread(d[k], rng, 2)
    return d
def setup_inputs_wide(rng):
    d = setup_inputs(rng)
    for k in ("wb",): d[k] = mx_ref.flush((d[k].astype(np.float32) * np.exp2(rng.integers(-6, 7, (N, 1, 1))).astype(np.float32)).astype(BF))
    return d
def setup_inputs_zeros(rng):
    d = setup_inputs(rng); v = d["x"].reshape(N, 128, -1, 4).copy()
    v[np.broadcast_to((rng.random((N, 1, v.shape[2], 1)) < 0.33), v.shape)] = 0
    d["x"] = v.reshape(d["x"].shape)
    return d
def reference(x, wa, wb):
    edge = lambda t, r: np.concatenate([t[(r - 1) % N][:, 4 * (NC - D):], t[r]], axis=1)
    u = [tile(act([taps(wa[r], i, edge(x, r)) for i in range(G)])) for r in range(N)]
    y = np.zeros((N, 128, NC), np.float32)
    for r in range(N):
        y[r] = taps(wb[r], 0, edge(u, r))
    return {"y": y}

@@ -1,0 +1,175 @@
+from concourse.bass import DstId, RemoteDMATransfer
+from concourse.mybir import dt, AluOpType, ActivationFunctionType
+
+D = 8
+H = 2 * D
+NC = 128
+NU = NC + D
+C = 0.031
+
+SCRATCH = {
+    "xb": ("sbuf", [128, 4 * NC], "bfloat16"),
+    "wab": ("sbuf", [128, 8 * 512], "bfloat16"),
+    "wbb": ("sbuf", [128, 2 * 512], "bfloat16"),
+    "e": ("sbuf", [128, H + NC], "float8_e4m3fn_x4"),
+    "es": ("sbuf", [128, 2 * H + NC], "uint8"),
+    "waq": ("sbuf", [128, 8 * 128], "float8_e4m3fn_x4"),
+    "was": ("sbuf", [128, 8 * 128], "uint8"),
+    "wbq": ("sbuf", [128, 2 * 128], "float8_e4m3fn_x4"),
+    "wbs": ("sbuf", [128, 2 * 128], "uint8"),
+    "u": ("sbuf", [128, 4 * NU], "bfloat16"),
+    "uq": ("sbuf", [128, NU], "float8_e4m3fn_x4"),
+    "us": ("sbuf", [128, NU], "uint8"),
+    "yb": ("sbuf", [128, NC], "float32"),
+    "rc": ("sbuf", [128, H], "float8_e4m3fn_x4"),
+    "rs": ("sbuf", [128, 2 * H], "uint8"),
+    "z": ("psum", [128, 4 * 512], "float32"),
+    "yp": ("psum", [128, 512], "float32"),
+}
+CHUNKS = [(0, 2), (2, 4), (4, 6), (6, 7), (7, 8)]
+SEMAPHORES = (["lx", "lb", "qx", "qb", "sent", "arr", "halo", "qu", "yd", "yc", "st"]
+              + ["lw%d" % k for k in range(len(CHUNKS))] + ["qw%d" % k for k in range(len(CHUNKS))]
+              + ["z%d" % i for i in range(4)] + ["r%d" % i for i in range(4)])
+KE = 4
+
+
+def engines(topo, src, dst, k, slot):
+    m = topo.mask(src, dst)
+    bits = [b for b in range(m.bit_length()) if (m >> b) & 1]
+    step = len(bits) // k
+    return sum(1 << b for b in bits[slot % step::step][:k])
+
+
+def dest(topo, c):
+    rid, pid, _ = topo.addr(c)
+    return [DstId(rid=rid, pnc=pid)]
+
+
+def relays(T, topo, src, dst):
+    if topo.may_write(src, dst):
+        return []
+    c = [k for k in range(src + 64) if topo.chip(k) == topo.chip(src) and T.rank_of(k) is None and topo.may_write(k, dst)]
+    c.sort(key=lambda k: (topo.die(k) != topo.die(src), k))
+    return [c[p % len(c)] for p in range(3)]
+
+
+def piece_src(T, p):
+    return [T.e[:, NC:NC + D].bitcast(dt.uint8), T.e[:, NC + D:NC + H].bitcast(dt.uint8), T.es[:, NC:NC + 2 * H]][p]
+
+
+def piece_relay(T, p):
+    return [T.rc[:, 0:D].bitcast(dt.uint8), T.rc[:, D:H].bitcast(dt.uint8), T.rs[:, 0:2 * H]][p]
+
+
+def piece_dst(T, p):
+    return [T.e[:, 0:D].bitcast(dt.uint8), T.e[:, D:H].bitcast(dt.uint8), T.es[:, 0:2 * H]][p]
+
+
+def relay_program(g, core, T, topo):
+    n = len(T.cores)
+    for r in range(n):
+        src, dst = T.cores[r], T.cores[(r + 1) % n]
+        for p, c in enumerate(relays(T, topo, src, dst)):
+            if c != core:
+                continue
+            rid, pid, _ = topo.addr(dst)
+            g.wait_ge(T.sem.arr, KE)
+            g.remote_dma(piece_dst(T, p), piece_relay(T, p), T.sem.halo, T.sem.sent, pid, rid, engines(topo, core, dst, KE, 0))
+            g.wait_ge(T.sem.sent, KE)
+
+
+def rank_program(g, core, T, topo):
+    rank = T.rank_of(core)
+    if rank is None:
+        relay_program(g, core, T, topo)
+        return
+    nxt = T.cores[(rank + 1) % len(T.cores)]
+    rel = relays(T, topo, core, nxt)
+    S = T.sem
+
+    def load_wa(q, k):
+        a, b = CHUNKS[k]
+        q.dma_start(T.wab[:, 512 * a:512 * b], T.wa[:, 512 * a:512 * b]).then_inc(S["lw%d" % k], 16)
+
+    def load_wb(q):
+        q.dma_start(T.wbb[:], T.wb[:]).then_inc(S.lb, 16)
+
+    g.sync.dma_start(T.xb[:], T.x[:]).then_inc(S.lx, 16)
+    if rel:
+        load_wa(g.sync, 0)
+        load_wa(g.sync, 1)
+        g.sync.wait_ge(S.sent, 3 * KE)
+        load_wa(g.sync, 2)
+        load_wb(g.sync)
+        load_wa(g.sync, 3)
+        load_wa(g.sync, 4)
+    else:
+        load_wa(g.scalar, 0)
+        load_wa(g.sync, 1)
+        load_wa(g.scalar, 2)
+        load_wb(g.sync)
+        load_wa(g.scalar, 3)
+        load_wa(g.sync, 4)
+
+    ts = []
+    for p in range(3):
+        to = rel[p] if rel else nxt
+        ts.append(RemoteDMATransfer(
+            dst_ids=dest(topo, to), dma_engine_mask=engines(topo, core, to, KE, p), remote_sem=S.arr if rel else S.halo,
+            src=piece_src(T, p), dst=piece_relay(T, p) if rel else piece_dst(T, p)))
+    g.wait_ge(S.qx, 1)
+    g.remote_dma_fused(ts, local_sem=S.sent)
+    if not rel:
+        g.wait_ge(S.sent, 3 * KE)
+
+    v = g.vector
+    v.wait_ge(S.lx, 16)
+    v.quantize_mx(T.e[:, H:H + NC], T.es[:, 2 * H:2 * H + NC], T.xb[:]).then_inc(S.qx, 1)
+
+    def quant_wa(k):
+        a, b = CHUNKS[k]
+        v.wait_ge(S["lw%d" % k], 16)
+        v.quantize_mx(T.waq[:, 128 * a:128 * b], T.was[:, 128 * a:128 * b], T.wab[:, 512 * a:512 * b]).then_inc(S["qw%d" % k], 1)
+
+    for k in (0, 1, 2):
+        quant_wa(k)
+    v.wait_ge(S.lb, 16)
+    v.quantize_mx(T.wbq[:], T.wbs[:], T.wbb[:]).then_inc(S.qb, 1)
+    for k in (3, 4):
+        quant_wa(k)
+    for i in (1, 3):
+        v.wait_ge(S["z%d" % i], 1)
+        v.tensor_scalar(T.u[:, i:4 * NU:4], T.z[:, 512 * i:512 * i + NU], 0.0, C, AluOpType.max, AluOpType.mult).then_inc(S["r%d" % i], 1)
+    for i in range(4):
+        v.wait_ge(S["r%d" % i], 1)
+    v.quantize_mx(T.uq[:], T.us[:], T.u[:]).then_inc(S.qu, 1)
+    v.wait_ge(S.yd, 1)
+    v.tensor_copy(T.yb[:], T.yp[:, 0:NC]).then_inc(S.yc, 1)
+
+    for i in (0, 2):
+        g.scalar.wait_ge(S["z%d" % i], 1)
+        g.scalar.activation(T.u[:, i:4 * NU:4], T.z[:, 512 * i:512 * i + NU], ActivationFunctionType.Relu, scale=C).then_inc(S["r%d" % i], 1)
+
+    t = g.tensor
+    t.wait_ge(S.qx, 1)
+    t.wait_ge(S.halo, 3 * KE)
+    for k, (a, b) in enumerate(CHUNKS):
+        t.wait_ge(S["qw%d" % k], 1)
+        for w in range(a, b):
+            i, tap = divmod(w, 2)
+            c = D * tap
+            mm = t.matmul_mx(T.z[:, 512 * i:512 * i + NU], T.waq[:, 128 * w:128 * w + 128], T.was[:, 128 * w:128 * w + 128],
+                             T.e[:, c:c + NU], T.es[:, H + c:H + c + NU], tap == 0, tap == 1)
+            if tap == 1:
+                mm.then_inc(S["z%d" % i], 1)
+    t.wait_ge(S.qb, 1)
+    t.wait_ge(S.qu, 1)
+    for tap in range(2):
+        c = D * tap
+        mm = t.matmul_mx(T.yp[:, 0:NC], T.wbq[:, 128 * tap:128 * tap + 128], T.wbs[:, 128 * tap:128 * tap + 128],
+                         T.uq[:, c:c + NC], T.us[:, c:c + NC], tap == 0, tap == 1)
+    mm.then_inc(S.yd, 1)
+
+    g.sync.wait_ge(S.yc, 1)
+    g.sync.dma_start(T.y[:], T.yb[:]).then_inc(S.st, 16)
+    g.sync.wait_ge(S.st, 16)

@@ -1,6 +1,7 @@
 from concourse.bass import DstId, RemoteDMATransfer
 from concourse.mybir import dt, AluOpType, ActivationFunctionType
 
+RELU, COPY = ActivationFunctionType.Relu, ActivationFunctionType.Copy
 D = 8
 H = 2 * D
 NC = 128
@@ -8,29 +9,34 @@ NU = NC + D
 C = 0.031
 
 SCRATCH = {
-    "xb": ("sbuf", [128, 4 * NC], "bfloat16"),
+    "xb": ("sbuf", [128, 4 * (NC + H)], "bfloat16"),
     "wab": ("sbuf", [128, 8 * 512], "bfloat16"),
     "wbb": ("sbuf", [128, 2 * 512], "bfloat16"),
-    "e": ("sbuf", [128, H + NC], "float8_e4m3fn_x4"),
-    "es": ("sbuf", [128, 2 * H + NC], "uint8"),
+    "e": ("sbuf", [128, H + NC + H], "float8_e4m3fn_x4"),
+    "es": ("sbuf", [128, 2 * H + NC + H], "uint8"),
     "waq": ("sbuf", [128, 8 * 128], "float8_e4m3fn_x4"),
     "was": ("sbuf", [128, 8 * 128], "uint8"),
     "wbq": ("sbuf", [128, 2 * 128], "float8_e4m3fn_x4"),
     "wbs": ("sbuf", [128, 2 * 128], "uint8"),
-    "u": ("sbuf", [128, 4 * NU], "bfloat16"),
+    "u": ("sbuf", [128, 4 * (H + NU)], "bfloat16"),
     "uq": ("sbuf", [128, NU], "float8_e4m3fn_x4"),
     "us": ("sbuf", [128, NU], "uint8"),
+    "uqm": ("sbuf", [128, NU], "float8_e4m3fn_x4"),
+    "usm": ("sbuf", [128, NU], "uint8"),
     "yb": ("sbuf", [128, NC], "float32"),
+    "ybm": ("sbuf", [128, NC - H], "float32"),
     "rc": ("sbuf", [128, H], "float8_e4m3fn_x4"),
-    "rs": ("sbuf", [128, 2 * H], "uint8"),
+    "rs": ("sbuf", [128, 4 * H], "uint8"),
     "z": ("psum", [128, 4 * 512], "float32"),
     "yp": ("psum", [128, 512], "float32"),
+    "ypm": ("psum", [128, 512], "float32"),
 }
 CHUNKS = [(0, 2), (2, 4), (4, 6), (6, 7), (7, 8)]
-SEMAPHORES = (["lx", "lb", "qx", "qb", "sent", "arr", "halo", "qu", "yd", "yc", "st"]
+SEMAPHORES = (["lx", "lb0", "lb1", "qx", "qb0", "qb1", "go", "sent", "arr", "halo", "qu", "yd", "yc", "st", "qum", "ydm", "ycm", "stm"]
               + ["lw%d" % k for k in range(len(CHUNKS))] + ["qw%d" % k for k in range(len(CHUNKS))]
-              + ["z%d" % i for i in range(4)] + ["r%d" % i for i in range(4)])
+              + ["%s%d" % (s, i) for s in ("z", "r", "zm", "rm") for i in range(4)])
 KE = 4
+KR = 4
 
 
 def engines(topo, src, dst, k, slot):
@@ -50,19 +56,23 @@ def relays(T, topo, src, dst):
         return []
     c = [k for k in range(src + 64) if topo.chip(k) == topo.chip(src) and T.rank_of(k) is None and topo.may_write(k, dst)]
     c.sort(key=lambda k: (topo.die(k) != topo.die(src), k))
-    return [c[p % len(c)] for p in range(3)]
+    return c[:2]
 
 
-def piece_src(T, p):
-    return [T.e[:, NC:NC + D].bitcast(dt.uint8), T.e[:, NC + D:NC + H].bitcast(dt.uint8), T.es[:, NC:NC + 2 * H]][p]
+def direct_pieces(T):
+    return [(T.e[:, NC:NC + D].bitcast(dt.uint8), T.e[:, 0:D].bitcast(dt.uint8)),
+            (T.e[:, NC + D:NC + H].bitcast(dt.uint8), T.e[:, D:H].bitcast(dt.uint8)),
+            (T.es[:, NC:NC + 2 * H], T.es[:, 0:2 * H])]
 
 
-def piece_relay(T, p):
-    return [T.rc[:, 0:D].bitcast(dt.uint8), T.rc[:, D:H].bitcast(dt.uint8), T.rs[:, 0:2 * H]][p]
+def relay_pieces(T):
+    return [(T.e[:, NC:NC + H].bitcast(dt.uint8), T.rc[:].bitcast(dt.uint8)),
+            (T.es[:, NC - 2 * H:NC + 2 * H], T.rs[:])]
 
 
-def piece_dst(T, p):
-    return [T.e[:, 0:D].bitcast(dt.uint8), T.e[:, D:H].bitcast(dt.uint8), T.es[:, 0:2 * H]][p]
+def passed_on(T):
+    return [(T.rc[:].bitcast(dt.uint8), T.e[:, 0:H].bitcast(dt.uint8)),
+            (T.rs[:, 3 * H:4 * H], T.es[:, H:2 * H])]
 
 
 def relay_program(g, core, T, topo):
@@ -73,9 +83,10 @@ def relay_program(g, core, T, topo):
             if c != core:
                 continue
             rid, pid, _ = topo.addr(dst)
+            a, b = passed_on(T)[p]
             g.wait_ge(T.sem.arr, KE)
-            g.remote_dma(piece_dst(T, p), piece_relay(T, p), T.sem.halo, T.sem.sent, pid, rid, engines(topo, core, dst, KE, 0))
-            g.wait_ge(T.sem.sent, KE)
+            g.remote_dma(b, a, T.sem.halo, T.sem.sent, pid, rid, engines(topo, core, dst, KR, 0))
+            g.wait_ge(T.sem.sent, KR)
 
 
 def rank_program(g, core, T, topo):
@@ -84,92 +95,131 @@ def rank_program(g, core, T, topo):
         relay_program(g, core, T, topo)
         return
     nxt = T.cores[(rank + 1) % len(T.cores)]
+    prv = T.cores[(rank - 1) % len(T.cores)]
     rel = relays(T, topo, core, nxt)
+    late = len(relays(T, topo, prv, core))
     S = T.sem
+    v, t, sc, sy = g.vector, g.tensor, g.scalar, g.sync
 
     def load_wa(q, k):
         a, b = CHUNKS[k]
         q.dma_start(T.wab[:, 512 * a:512 * b], T.wa[:, 512 * a:512 * b]).then_inc(S["lw%d" % k], 16)
 
-    def load_wb(q):
-        q.dma_start(T.wbb[:], T.wb[:]).then_inc(S.lb, 16)
+    def load_wb(q, k):
+        q.dma_start(T.wbb[:, 512 * k:512 * k + 512], T.wb[:, 512 * k:512 * k + 512]).then_inc(S["lb%d" % k], 16)
 
-    g.sync.dma_start(T.xb[:], T.x[:]).then_inc(S.lx, 16)
+    spare = H if late else 0
+    sy.dma_start(T.xb[:, 0:4 * NC], T.x[:]).then_inc(S.lx, 16)
+    if spare:
+        sy.dma_start(T.xb[:, 4 * NC:4 * (NC + spare)], T.x[:, 0:4 * spare]).then_inc(S.lx, 16)
+    q2 = sy if rel else sc
+    load_wa(q2, 0)
+    load_wa(sy, 1)
     if rel:
-        load_wa(g.sync, 0)
-        load_wa(g.sync, 1)
-        g.sync.wait_ge(S.sent, 3 * KE)
-        load_wa(g.sync, 2)
-        load_wb(g.sync)
-        load_wa(g.sync, 3)
-        load_wa(g.sync, 4)
-    else:
-        load_wa(g.scalar, 0)
-        load_wa(g.sync, 1)
-        load_wa(g.scalar, 2)
-        load_wb(g.sync)
-        load_wa(g.scalar, 3)
-        load_wa(g.sync, 4)
+        sy.wait_ge(S.go, 1)
+    load_wa(q2, 2)
+    load_wa(sy, 3)
+    load_wa(q2, 4)
+    load_wb(sy, 0)
+    load_wb(q2, 1)
 
     ts = []
-    for p in range(3):
+    for p, (a, b) in enumerate(relay_pieces(T) if rel else direct_pieces(T)):
         to = rel[p] if rel else nxt
-        ts.append(RemoteDMATransfer(
-            dst_ids=dest(topo, to), dma_engine_mask=engines(topo, core, to, KE, p), remote_sem=S.arr if rel else S.halo,
-            src=piece_src(T, p), dst=piece_relay(T, p) if rel else piece_dst(T, p)))
+        ts.append(RemoteDMATransfer(dst_ids=dest(topo, to), dma_engine_mask=engines(topo, core, to, KE, p),
+                                    remote_sem=S.arr if rel else S.halo, src=a, dst=b))
     g.wait_ge(S.qx, 1)
     g.remote_dma_fused(ts, local_sem=S.sent)
-    if not rel:
-        g.wait_ge(S.sent, 3 * KE)
+    if rel:
+        g.sem_inc(S.go, 1)
+    g.wait_ge(S.sent, len(ts) * KE)
 
-    v = g.vector
-    v.wait_ge(S.lx, 16)
-    v.quantize_mx(T.e[:, H:H + NC], T.es[:, 2 * H:2 * H + NC], T.xb[:]).then_inc(S.qx, 1)
+    def quant_wb(k):
+        v.wait_ge(S["lb%d" % k], 16)
+        v.quantize_mx(T.wbq[:, 128 * k:128 * k + 128], T.wbs[:, 128 * k:128 * k + 128], T.wbb[:, 512 * k:512 * k + 512]).then_inc(S["qb%d" % k], 1)
 
-    def quant_wa(k):
-        a, b = CHUNKS[k]
+    def mm_z(w, first, n, sem):
+        i, tap = divmod(w, 2)
+        c = first + D * tap
+        m = t.matmul_mx(T.z[:, 512 * i:512 * i + n], T.waq[:, 128 * w:128 * w + 128], T.was[:, 128 * w:128 * w + 128],
+                        T.e[:, c:c + n], T.es[:, H + c:H + c + n], tap == 0, tap == 1)
+        if tap == 1:
+            m.then_inc(S["%s%d" % (sem, i)], 1)
+
+    def mm_y(out, uq, us, sem):
+        for tap in range(2):
+            c = D * tap
+            t.wait_ge(S["qb%d" % tap], 1)
+            m = t.matmul_mx(out[:, 0:NC], T.wbq[:, 128 * tap:128 * tap + 128], T.wbs[:, 128 * tap:128 * tap + 128],
+                            uq[:, c:c + NC], us[:, c:c + NC], tap == 0, tap == 1)
+        m.then_inc(sem, 1)
+
+    def act(eng, i, first, n, zs, rs):
+        eng.wait_ge(S["%s%d" % (zs, i)], 1)
+        out, z = T.u[:, 4 * first + i:4 * (first + n):4], T.z[:, 512 * i:512 * i + n]
+        if eng is v:
+            c = v.tensor_scalar(out, z, 0.0, C, AluOpType.max, AluOpType.mult)
+        else:
+            c = sc.activation(out, z, RELU, scale=C)
+        c.then_inc(S["%s%d" % (rs, i)], 1)
+
+    v.wait_ge(S.lx, 32 if spare else 16)
+    v.quantize_mx(T.e[:, H:H + NC + spare], T.es[:, 2 * H:2 * H + NC + spare], T.xb[:, 0:4 * (NC + spare)]).then_inc(S.qx, 1)
+    for k, (a, b) in enumerate(CHUNKS):
         v.wait_ge(S["lw%d" % k], 16)
         v.quantize_mx(T.waq[:, 128 * a:128 * b], T.was[:, 128 * a:128 * b], T.wab[:, 512 * a:512 * b]).then_inc(S["qw%d" % k], 1)
+    quant_wb(0)
 
-    for k in (0, 1, 2):
-        quant_wa(k)
-    v.wait_ge(S.lb, 16)
-    v.quantize_mx(T.wbq[:], T.wbs[:], T.wbb[:]).then_inc(S.qb, 1)
-    for k in (3, 4):
-        quant_wa(k)
-    for i in (1, 3):
-        v.wait_ge(S["z%d" % i], 1)
-        v.tensor_scalar(T.u[:, i:4 * NU:4], T.z[:, 512 * i:512 * i + NU], 0.0, C, AluOpType.max, AluOpType.mult).then_inc(S["r%d" % i], 1)
+    t.wait_ge(S.qx, 1)
+    if late:
+        for k, (a, b) in enumerate(CHUNKS):
+            t.wait_ge(S["qw%d" % k], 1)
+            for w in range(a, b):
+                mm_z(w, H, NU, "zm")
+        t.wait_ge(S.halo, late * KR)
+        for w in range(8):
+            if w % 2 == 0:
+                t.wait_ge(S["rm%d" % (w // 2)], 1)
+            mm_z(w, 0, NC, "z")
+        t.wait_ge(S.qum, 1)
+        mm_y(T.ypm, T.uqm, T.usm, S.ydm)
+        t.wait_ge(S.qu, 1)
+        mm_y(T.yp, T.uq, T.us, S.yd)
+        for i in range(4):
+            act(sc, i, H, NU, "zm", "rm")
+        sc.wait_ge(S.ydm, 1)
+        sc.activation(T.ybm[:], T.ypm[:, 0:NC - H], COPY).then_inc(S.ycm, 1)
+        sc.wait_ge(S.ycm, 1)
+        sc.dma_start(T.y[:, H:NC], T.ybm[:]).then_inc(S.stm, 16)
+        sc.wait_ge(S.stm, 16)
+        for i in range(4):
+            v.wait_ge(S["rm%d" % i], 1)
+        v.quantize_mx(T.uqm[:], T.usm[:], T.u[:, 4 * H:4 * (H + NU)]).then_inc(S.qum, 1)
+        act(v, 0, 0, H, "z", "r")
+        act(v, 1, 0, H, "z", "r")
+        quant_wb(1)
+        act(v, 2, 0, H, "z", "r")
+        act(v, 3, 0, H, "z", "r")
+        ny = H
+    else:
+        t.wait_ge(S.halo, len(direct_pieces(T)) * KE)
+        for k, (a, b) in enumerate(CHUNKS):
+            t.wait_ge(S["qw%d" % k], 1)
+            for w in range(a, b):
+                mm_z(w, 0, NU, "z")
+        t.wait_ge(S.qu, 1)
+        mm_y(T.yp, T.uq, T.us, S.yd)
+        for i in (0, 2, 3):
+            act(sc, i, 0, NU, "z", "r")
+        act(v, 1, 0, NU, "z", "r")
+        ny = NC
     for i in range(4):
         v.wait_ge(S["r%d" % i], 1)
-    v.quantize_mx(T.uq[:], T.us[:], T.u[:]).then_inc(S.qu, 1)
+    v.quantize_mx(T.uq[:], T.us[:], T.u[:, 0:4 * NU]).then_inc(S.qu, 1)
+    if not late:
+        quant_wb(1)
     v.wait_ge(S.yd, 1)
-    v.tensor_copy(T.yb[:], T.yp[:, 0:NC]).then_inc(S.yc, 1)
-
-    for i in (0, 2):
-        g.scalar.wait_ge(S["z%d" % i], 1)
-        g.scalar.activation(T.u[:, i:4 * NU:4], T.z[:, 512 * i:512 * i + NU], ActivationFunctionType.Relu, scale=C).then_inc(S["r%d" % i], 1)
-
-    t = g.tensor
-    t.wait_ge(S.qx, 1)
-    t.wait_ge(S.halo, 3 * KE)
-    for k, (a, b) in enumerate(CHUNKS):
-        t.wait_ge(S["qw%d" % k], 1)
-        for w in range(a, b):
-            i, tap = divmod(w, 2)
-            c = D * tap
-            mm = t.matmul_mx(T.z[:, 512 * i:512 * i + NU], T.waq[:, 128 * w:128 * w + 128], T.was[:, 128 * w:128 * w + 128],
-                             T.e[:, c:c + NU], T.es[:, H + c:H + c + NU], tap == 0, tap == 1)
-            if tap == 1:
-                mm.then_inc(S["z%d" % i], 1)
-    t.wait_ge(S.qb, 1)
-    t.wait_ge(S.qu, 1)
-    for tap in range(2):
-        c = D * tap
-        mm = t.matmul_mx(T.yp[:, 0:NC], T.wbq[:, 128 * tap:128 * tap + 128], T.wbs[:, 128 * tap:128 * tap + 128],
-                         T.uq[:, c:c + NC], T.us[:, c:c + NC], tap == 0, tap == 1)
-    mm.then_inc(S.yd, 1)
-
-    g.sync.wait_ge(S.yc, 1)
-    g.sync.dma_start(T.y[:], T.yb[:]).then_inc(S.st, 16)
-    g.sync.wait_ge(S.st, 16)
+    v.tensor_copy(T.yb[:, 0:ny], T.yp[:, 0:ny]).then_inc(S.yc, 1)
+    sy.wait_ge(S.yc, 1)
+    sy.dma_start(T.y[:, 0:ny], T.yb[:, 0:ny]).then_inc(S.st, 16)
+    sy.wait_ge(S.st, 16)

from concourse.bass import DstId, RemoteDMATransfer
from concourse.mybir import dt, AluOpType, ActivationFunctionType

RELU, COPY = ActivationFunctionType.Relu, ActivationFunctionType.Copy
D = 8
H = 2 * D
NC = 128
NU = NC + D
C = 0.031

SCRATCH = {
    "xb": ("sbuf", [128, 4 * (NC + H)], "bfloat16"),
    "wab": ("sbuf", [128, 8 * 512], "bfloat16"),
    "wbb": ("sbuf", [128, 2 * 512], "bfloat16"),
    "e": ("sbuf", [128, H + NC + H], "float8_e4m3fn_x4"),
    "es": ("sbuf", [128, 2 * H + NC + H], "uint8"),
    "waq": ("sbuf", [128, 8 * 128], "float8_e4m3fn_x4"),
    "was": ("sbuf", [128, 8 * 128], "uint8"),
    "wbq": ("sbuf", [128, 2 * 128], "float8_e4m3fn_x4"),
    "wbs": ("sbuf", [128, 2 * 128], "uint8"),
    "u": ("sbuf", [128, 4 * (H + NU)], "bfloat16"),
    "uq": ("sbuf", [128, NU], "float8_e4m3fn_x4"),
    "us": ("sbuf", [128, NU], "uint8"),
    "uqm": ("sbuf", [128, NU], "float8_e4m3fn_x4"),
    "usm": ("sbuf", [128, NU], "uint8"),
    "yb": ("sbuf", [128, NC], "float32"),
    "ybm": ("sbuf", [128, NC - H], "float32"),
    "rc": ("sbuf", [128, H], "float8_e4m3fn_x4"),
    "rs": ("sbuf", [128, 4 * H], "uint8"),
    "z": ("psum", [128, 4 * 512], "float32"),
    "yp": ("psum", [128, 512], "float32"),
    "ypm": ("psum", [128, 512], "float32"),
}
CHUNKS = [(0, 2), (2, 4), (4, 6), (6, 7), (7, 8)]
SEMAPHORES = (["lx", "lb0", "lb1", "qx", "qb0", "qb1", "go", "sent", "arr", "halo", "qu", "yd", "yc", "st", "qum", "ydm", "ycm", "stm"]
              + ["lw%d" % k for k in range(len(CHUNKS))] + ["qw%d" % k for k in range(len(CHUNKS))]
              + ["%s%d" % (s, i) for s in ("z", "r", "zm", "rm") for i in range(4)])
KE = 4
KR = 4


def engines(topo, src, dst, k, slot):
    m = topo.mask(src, dst)
    bits = [b for b in range(m.bit_length()) if (m >> b) & 1]
    step = len(bits) // k
    return sum(1 << b for b in bits[slot % step::step][:k])


def dest(topo, c):
    rid, pid, _ = topo.addr(c)
    return [DstId(rid=rid, pnc=pid)]


def relays(T, topo, src, dst):
    if topo.may_write(src, dst):
        return []
    c = [k for k in range(src + 64) if topo.chip(k) == topo.chip(src) and T.rank_of(k) is None and topo.may_write(k, dst)]
    c.sort(key=lambda k: (topo.die(k) != topo.die(src), k))
    return c[:2]


def direct_pieces(T):
    return [(T.e[:, NC:NC + D].bitcast(dt.uint8), T.e[:, 0:D].bitcast(dt.uint8)),
            (T.e[:, NC + D:NC + H].bitcast(dt.uint8), T.e[:, D:H].bitcast(dt.uint8)),
            (T.es[:, NC:NC + 2 * H], T.es[:, 0:2 * H])]


def relay_pieces(T):
    return [(T.e[:, NC:NC + H].bitcast(dt.uint8), T.rc[:].bitcast(dt.uint8)),
            (T.es[:, NC - 2 * H:NC + 2 * H], T.rs[:])]


def passed_on(T):
    return [(T.rc[:].bitcast(dt.uint8), T.e[:, 0:H].bitcast(dt.uint8)),
            (T.rs[:, 3 * H:4 * H], T.es[:, H:2 * H])]


def relay_program(g, core, T, topo):
    n = len(T.cores)
    for r in range(n):
        src, dst = T.cores[r], T.cores[(r + 1) % n]
        for p, c in enumerate(relays(T, topo, src, dst)):
            if c != core:
                continue
            rid, pid, _ = topo.addr(dst)
            a, b = passed_on(T)[p]
            g.wait_ge(T.sem.arr, KE)
            g.remote_dma(b, a, T.sem.halo, T.sem.sent, pid, rid, engines(topo, core, dst, KR, 0))
            g.wait_ge(T.sem.sent, KR)


def rank_program(g, core, T, topo):
    rank = T.rank_of(core)
    if rank is None:
        relay_program(g, core, T, topo)
        return
    nxt = T.cores[(rank + 1) % len(T.cores)]
    prv = T.cores[(rank - 1) % len(T.cores)]
    rel = relays(T, topo, core, nxt)
    late = len(relays(T, topo, prv, core))
    S = T.sem
    v, t, sc, sy = g.vector, g.tensor, g.scalar, g.sync

    def load_wa(q, k):
        a, b = CHUNKS[k]
        q.dma_start(T.wab[:, 512 * a:512 * b], T.wa[:, 512 * a:512 * b]).then_inc(S["lw%d" % k], 16)

    def load_wb(q, k):
        q.dma_start(T.wbb[:, 512 * k:512 * k + 512], T.wb[:, 512 * k:512 * k + 512]).then_inc(S["lb%d" % k], 16)

    spare = H if late else 0
    sy.dma_start(T.xb[:, 0:4 * NC], T.x[:]).then_inc(S.lx, 16)
    if spare:
        sy.dma_start(T.xb[:, 4 * NC:4 * (NC + spare)], T.x[:, 0:4 * spare]).then_inc(S.lx, 16)
    q2 = sy if rel else sc
    load_wa(q2, 0)
    load_wa(sy, 1)
    if rel:
        sy.wait_ge(S.go, 1)
    load_wa(q2, 2)
    load_wa(sy, 3)
    load_wa(q2, 4)
    load_wb(sy, 0)
    load_wb(q2, 1)

    ts = []
    for p, (a, b) in enumerate(relay_pieces(T) if rel else direct_pieces(T)):
        to = rel[p] if rel else nxt
        ts.append(RemoteDMATransfer(dst_ids=dest(topo, to), dma_engine_mask=engines(topo, core, to, KE, p),
                                    remote_sem=S.arr if rel else S.halo, src=a, dst=b))
    g.wait_ge(S.qx, 1)
    g.remote_dma_fused(ts, local_sem=S.sent)
    if rel:
        g.sem_inc(S.go, 1)
    g.wait_ge(S.sent, len(ts) * KE)

    def quant_wb(k):
        v.wait_ge(S["lb%d" % k], 16)
        v.quantize_mx(T.wbq[:, 128 * k:128 * k + 128], T.wbs[:, 128 * k:128 * k + 128], T.wbb[:, 512 * k:512 * k + 512]).then_inc(S["qb%d" % k], 1)

    def mm_z(w, first, n, sem):
        i, tap = divmod(w, 2)
        c = first + D * tap
        m = t.matmul_mx(T.z[:, 512 * i:512 * i + n], T.waq[:, 128 * w:128 * w + 128], T.was[:, 128 * w:128 * w + 128],
                        T.e[:, c:c + n], T.es[:, H + c:H + c + n], tap == 0, tap == 1)
        if tap == 1:
            m.then_inc(S["%s%d" % (sem, i)], 1)

    def mm_y(out, uq, us, sem):
        for tap in range(2):
            c = D * tap
            t.wait_ge(S["qb%d" % tap], 1)
            m = t.matmul_mx(out[:, 0:NC], T.wbq[:, 128 * tap:128 * tap + 128], T.wbs[:, 128 * tap:128 * tap + 128],
                            uq[:, c:c + NC], us[:, c:c + NC], tap == 0, tap == 1)
        m.then_inc(sem, 1)

    def act(eng, i, first, n, zs, rs):
        eng.wait_ge(S["%s%d" % (zs, i)], 1)
        out, z = T.u[:, 4 * first + i:4 * (first + n):4], T.z[:, 512 * i:512 * i + n]
        if eng is v:
            c = v.tensor_scalar(out, z, 0.0, C, AluOpType.max, AluOpType.mult)
        else:
            c = sc.activation(out, z, RELU, scale=C)
        c.then_inc(S["%s%d" % (rs, i)], 1)

    v.wait_ge(S.lx, 32 if spare else 16)
    v.quantize_mx(T.e[:, H:H + NC + spare], T.es[:, 2 * H:2 * H + NC + spare], T.xb[:, 0:4 * (NC + spare)]).then_inc(S.qx, 1)
    for k, (a, b) in enumerate(CHUNKS):
        v.wait_ge(S["lw%d" % k], 16)
        v.quantize_mx(T.waq[:, 128 * a:128 * b], T.was[:, 128 * a:128 * b], T.wab[:, 512 * a:512 * b]).then_inc(S["qw%d" % k], 1)
    quant_wb(0)

    t.wait_ge(S.qx, 1)
    if late:
        for k, (a, b) in enumerate(CHUNKS):
            t.wait_ge(S["qw%d" % k], 1)
            for w in range(a, b):
                mm_z(w, H, NU, "zm")
        t.wait_ge(S.halo, late * KR)
        for w in range(8):
            if w % 2 == 0:
                t.wait_ge(S["rm%d" % (w // 2)], 1)
            mm_z(w, 0, NC, "z")
        t.wait_ge(S.qum, 1)
        mm_y(T.ypm, T.uqm, T.usm, S.ydm)
        t.wait_ge(S.qu, 1)
        mm_y(T.yp, T.uq, T.us, S.yd)
        for i in range(4):
            act(sc, i, H, NU, "zm", "rm")
        sc.wait_ge(S.ydm, 1)
        sc.activation(T.ybm[:], T.ypm[:, 0:NC - H], COPY).then_inc(S.ycm, 1)
        sc.wait_ge(S.ycm, 1)
        sc.dma_start(T.y[:, H:NC], T.ybm[:]).then_inc(S.stm, 16)
        sc.wait_ge(S.stm, 16)
        for i in range(4):
            v.wait_ge(S["rm%d" % i], 1)
        v.quantize_mx(T.uqm[:], T.usm[:], T.u[:, 4 * H:4 * (H + NU)]).then_inc(S.qum, 1)
        act(v, 0, 0, H, "z", "r")
        act(v, 1, 0, H, "z", "r")
        quant_wb(1)
        act(v, 2, 0, H, "z", "r")
        act(v, 3, 0, H, "z", "r")
        ny = H
    else:
        t.wait_ge(S.halo, len(direct_pieces(T)) * KE)
        for k, (a, b) in enumerate(CHUNKS):
            t.wait_ge(S["qw%d" % k], 1)
            for w in range(a, b):
                mm_z(w, 0, NU, "z")
        t.wait_ge(S.qu, 1)
        mm_y(T.yp, T.uq, T.us, S.yd)
        for i in (0, 2, 3):
            act(sc, i, 0, NU, "z", "r")
        act(v, 1, 0, NU, "z", "r")
        ny = NC
    for i in range(4):
        v.wait_ge(S["r%d" % i], 1)
    v.quantize_mx(T.uq[:], T.us[:], T.u[:, 0:4 * NU]).then_inc(S.qu, 1)
    if not late:
        quant_wb(1)
    v.wait_ge(S.yd, 1)
    v.tensor_copy(T.yb[:, 0:ny], T.yp[:, 0:ny]).then_inc(S.yc, 1)
    sy.wait_ge(S.yc, 1)
    sy.dma_start(T.y[:, 0:ny], T.yb[:, 0:ny]).then_inc(S.st, 16)
    sy.wait_ge(S.st, 16)
